import numpy as np
import ml_dtypes


def mxq(x, axis, fmt="e4m3"):
    dtype, down = {"e4m3": (ml_dtypes.float8_e4m3fn, 7), "e5m2": (ml_dtypes.float8_e5m2, 14)}[fmt]
    v = np.moveaxis(np.asarray(x, np.float32).astype(ml_dtypes.bfloat16).astype(np.float64), axis, -1)
    blocks = v.reshape(v.shape[:-1] + (-1, 32))
    amax = np.abs(blocks).max(-1, keepdims=True)
    byte = np.maximum(np.where(amax > 0, np.frexp(amax)[1] - 1 + 127, 0) - down, 1)
    scale = np.exp2(byte - 127.0)
    codes = (blocks / scale).astype(np.float32).astype(dtype).astype(np.float64)
    return np.moveaxis((codes * scale).reshape(v.shape), -1, axis)


WIDE = False


def mx_kscale(k):
    if not WIDE:
        return np.ones(k)
    levels = np.array([10, -10, 5, -5, 0])
    if k % 512:
        return np.exp2(np.random.permutation(np.resize(levels, k // 32))).repeat(32)
    a = np.empty((k // 512, 16))
    for p in range(k // 512):
        a[p, :8] = np.random.permutation(np.resize(levels, 8))
        for g in range(8):
            far = levels[np.abs(levels - a[p, g]) >= 10]
            a[p, g + 8] = far[np.random.randint(len(far))]
    return np.exp2(a.ravel()).repeat(32)


def f64(x):
    return np.asarray(x).astype(np.float64)


def striped(idx):
    return np.tile(idx.reshape(-1, 16).T, (8, 1)).astype(np.uint16)


def unstriped(offs):
    return offs[:16].T.reshape(-1).astype(np.int64)


def striped8(idx):
    return np.concatenate([x.reshape(-1, 16).T for x in idx]).astype(np.uint16)


def runs(offs, k):
    lists = np.stack([offs[16 * r : 16 * r + 16].T.reshape(-1) for r in range(8)]).astype(np.int64)
    return lists[np.arange(k) % 512 // 64]


def pack_weight(w):
    k, n = w.shape
    w = f64(np.asarray(w, np.float32).astype(ml_dtypes.bfloat16)).reshape(k // 32, 32, n)
    amax = np.abs(w).max(1)
    byte = np.clip(np.where(amax > 0, np.frexp(amax)[1] - 1 + 127 - 7, 1), 1, 254)
    scaled = (w * np.exp2(127.0 - byte)[:, None, :]).reshape(k, n).astype(np.float32)
    words = np.ascontiguousarray(scaled.reshape(k // 512, 128, 4, n).transpose(0, 1, 3, 2)).astype(ml_dtypes.float8_e4m3fn).view(np.uint8)
    return words, np.ascontiguousarray(byte.astype(np.uint8).reshape(k // 512, 16, n))


def unpack_weight(words, scales):
    g, p, n, _ = words.shape
    vals = np.ascontiguousarray(words).view(ml_dtypes.float8_e4m3fn).astype(np.float64) * np.repeat(np.exp2(scales.astype(np.float64) - 127.0), 8, axis=1)[..., None]
    return vals.transpose(0, 1, 3, 2).reshape(g * 512, n)

def planes(y):
    n, m = y.shape
    v = y.astype(np.float32).astype(ml_dtypes.bfloat16).astype(np.float64).reshape(n // 32, 32, m)
    top = np.abs(v).max(1)
    byte = np.clip(np.where(top > 0, np.frexp(top)[1] - 1 + 127 - 7, 1), 1, 254)
    codes = (v * np.exp2(127.0 - byte)[:, None, :]).reshape(n, m).astype(np.float32).astype(ml_dtypes.float8_e4m3fn).view(np.uint8)
    words = codes.reshape(n // 512, 128, 4, m).transpose(0, 1, 3, 2)
    return np.ascontiguousarray(words), np.ascontiguousarray(byte.astype(np.uint8).reshape(n // 512, 16, m))


K, T, S, N, H, W = 512, 2048, 512, 512, 512, 2048


def setup_inputs():
    n = np.random.standard_normal
    s = mx_kscale(K)[:, None]
    u = mx_kscale(H)
    packed_xT = pack_weight(n((K, T)) * s)
    packed_w1 = pack_weight(n((K, H)) / np.sqrt(K) / s)
    packed_w2 = pack_weight(n((H, N)) / np.sqrt(2 * H) / u[:, None])
    packed_w3 = pack_weight(n((K, N)) / np.sqrt(2 * K) / s)
    return {
        "x_words": packed_xT[0],
        "x_scales": packed_xT[1],
        "w1_words": packed_w1[0],
        "w1_scales": packed_w1[1],
        "gn": (np.random.uniform(0.5, 1.5, (H, 1)) * u[:, None]).astype(np.float32),
        "w2_words": packed_w2[0],
        "w2_scales": packed_w2[1],
        "w3_words": packed_w3[0],
        "w3_scales": packed_w3[1],
        "offs": striped(np.random.permutation(T)[:S]),
        "n1": striped(np.random.randint(0, S, W)),
        "hz": striped8(np.random.randint(0, T, (8, S))),
        "n2": striped8(np.stack([np.random.permutation(S) for _ in range(8)])),
        "n3": striped8(np.stack([np.random.permutation(S) for _ in range(8)])),
    }


def reference(x_words, x_scales, w1_words, w1_scales, gn, w2_words, w2_scales, w3_words, w3_scales, offs, n1, hz, n2, n3):
    xq = unpack_weight(x_words, x_scales)[:, unstriped(offs)]
    y = unpack_weight(w1_words, w1_scales).T @ xq
    ex = np.exp(0.5 * y)
    mb = ex[:, unstriped(n1)]
    ms = mb.reshape(H, S, 4).sum(axis=2)
    z = f64(gn) * ((4.0 * ex) / (ms + 0.5))
    x_hz = unpack_weight(x_words, x_scales)[np.arange(K)[:, None], runs(hz, K)]
    h = unpack_weight(w2_words, w2_scales).T @ mxq(z, 0, "e4m3") + unpack_weight(w3_words, w3_scales).T @ x_hz
    out_0 = h[np.arange(N)[:, None], runs(n2, N)] - (h[np.arange(N)[:, None], runs(n3, N)])
    return (out_0,) + planes(out_0)

@@ -1,0 +1,239 @@
+from contextlib import ExitStack
+
+import concourse.mybir as mybir
+
+K, T, S, H, N = 512, 2048, 512, 512, 512
+FLOPS = 3 * 2 * 512 * 512 * 512
+
+F32 = mybir.dt.float32
+BF16 = mybir.dt.bfloat16
+I32 = mybir.dt.int32
+U32 = mybir.dt.uint32
+U16 = mybir.dt.uint16
+U8 = mybir.dt.uint8
+FP8X4 = mybir.dt.float8_e4m3fn_x4
+ACT = mybir.ActivationFunctionType
+ALU = mybir.AluOpType
+
+P = 128
+PACK = 4
+MEMBERS = 4
+PER_COL = 16
+SPARE = 32
+CHUNK = 128
+CHUNKS = S // CHUNK
+VECTOR_TILES = ((0, 1, 2), (0, 1), (), ())
+OUT_CHUNKS = (256, 128, 128)
+RUN = 4
+
+
+def words_of(dram_words):
+    return dram_words[0].rearrange("p c r -> p (c r)").bitcast(I32)
+
+
+def load_scale_rows(queues, plane, first, dram_scales):
+    rows = dram_scales[0].bitcast(I32)
+    for q in range(4):
+        queues[q].dma_start(out=plane[32 * q + first : 32 * q + first + 4, :].bitcast(I32), in_=rows[4 * q : 4 * q + 4, :])
+
+
+def deal_columns(nc, dealt, raw):
+    nc.vector.tensor_copy(out=dealt.rearrange("p (t m) -> p t m", t=PACK), in_=raw.rearrange("p (m t) -> p t m", t=PACK))
+
+
+def tile_picked_mixhgsharegap_none_po_kernel(
+    tc, x_words, x_scales, w1_words, w1_scales, gn, w2_words, w2_scales, w3_words, w3_scales,
+    offs, n1, hz, n2, n3, out_0, out_1, out_2,
+):
+    nc = tc.nc
+    with ExitStack() as ctx:
+        keep = ctx.enter_context(tc.tile_pool(name="keep", bufs=1))
+        psum = ctx.enter_context(tc.psum_pool(name="psum", bufs=1))
+
+        def sb(name, shape, dtype):
+            return keep.tile(shape, dtype, name=name, align_bytes=64)
+
+        offs_sb = sb("offs_sb", [P, S // PER_COL], U16)
+        hz_sb = sb("hz_sb", [P, S // PER_COL], U16)
+        n1_sb = sb("n1_sb", [P, MEMBERS * S // PER_COL], U16)
+        n2_sb = sb("n2_sb", [P, S // PER_COL], U16)
+        n3_sb = sb("n3_sb", [P, S // PER_COL], U16)
+        xw = sb("xw", [P, T], U32)
+        xs = sb("xs", [P, T], U8)
+        xs_runs = sb("xs_runs", [P, T], U8)
+        w_raw = sb("w_raw", [P, H], U32)
+        ws_raw = sb("ws_raw", [P, H], U8)
+        gn_sb = sb("gn_sb", [P, PACK], F32)
+        zeros = sb("zeros", [P, SPARE], F32)
+
+        nc.gpsimd.memset(xs[:].bitcast(I32), 0)
+        nc.gpsimd.memset(ws_raw[:].bitcast(I32), 0)
+        nc.gpsimd.memset(zeros[:], 0.0)
+
+        for tile, dram in ((offs_sb, offs), (hz_sb, hz), (n1_sb, n1), (n3_sb, n3), (n2_sb, n2)):
+            nc.sync.dma_start(tile[:], dram)
+        nc.sync.dma_start(out=w_raw[:].bitcast(I32), in_=words_of(w1_words))
+        nc.sync.dma_start(out=xw[:].bitcast(I32), in_=words_of(x_words))
+        load_scale_rows([nc.scalar] * 4, xs, 0, x_scales)
+        load_scale_rows([nc.scalar] * 3 + [nc.gpsimd], ws_raw, 0, w1_scales)
+        nc.gpsimd.memset(xs_runs[:].bitcast(I32), 0)
+        nc.scalar.dma_start(out=gn_sb[:], in_=gn.rearrange("(p t) o -> p (t o)", t=PACK))
+        x_rows = x_scales[0].bitcast(I32)
+        for e in range(2):
+            nc.sync.dma_start(out=xs_runs[e:P:16, :].bitcast(I32), in_=x_rows[e:16:2, :])
+
+        ex = [sb("ex%d" % t, [P, S + SPARE], F32) for t in range(PACK)]
+        for t in range(PACK):
+            nc.scalar.activation(out=ex[t][:, S:], in_=zeros[:], func=ACT.Copy)
+
+        xq_s = sb("xq_s", [P, S], U8)
+        xq_w = sb("xq_w", [P, S], U32)
+        w1 = sb("w1", [P, H], U32)
+        w1s = sb("w1s", [P, H], U8)
+        nc.vector.tensor_copy(out=xq_s[:], in_=xs[:].indirect(offs_sb[:]))
+        deal_columns(nc, w1[:].bitcast(I32), w_raw[:].bitcast(I32))
+        nc.vector.tensor_copy(out=xq_w[:], in_=xw[:].indirect(offs_sb[:]))
+        deal_columns(nc, w1s[:], ws_raw[:])
+        nc.sync.dma_start(out=w_raw[:].bitcast(I32), in_=words_of(w3_words))
+        load_scale_rows([nc.sync] * 4, ws_raw, 4, w3_scales)
+        load_scale_rows([nc.sync] * 4, ws_raw, 8, w2_scales)
+
+        for t in range(PACK):
+            cols = slice(t * P, (t + 1) * P)
+            y = psum.tile([P, S], F32, name="y%d" % t)
+            nc.tensor.matmul_mx(
+                out=y[:], lhsT=w1[:, cols].bitcast(FP8X4), lhsT_scale=w1s[:, cols],
+                rhs=xq_w[:].bitcast(FP8X4), rhs_scale=xq_s[:], start=True, stop=True,
+            )
+            nc.scalar.activation(out=ex[t][:, :S], in_=y[:], func=ACT.Exp, scale=0.5)
+
+        xh_w = sb("xh_w", [P, S], U32)
+        xh_runs = sb("xh_runs", [P, S], U8)
+        xh_s = sb("xh_s", [P, S], U8)
+        nc.vector.tensor_copy(out=xh_w[:], in_=xw[:].indirect(hz_sb[:]))
+
+        w2 = sb("w2", [P, N], U32)
+        w3 = sb("w3", [P, N], U32)
+        w23s = sb("w23s", [P, N], U8)
+
+        deal_columns(nc, w3[:].bitcast(I32), w_raw[:].bitcast(I32))
+        nc.sync.dma_start(out=w_raw[:].bitcast(I32), in_=words_of(w2_words))
+
+        def prepare_second_layer():
+            nc.vector.tensor_copy(out=xh_runs[:], in_=xs_runs[:].indirect(hz_sb[:]))
+            nc.vector.tensor_copy(out=xh_s[:].bitcast(I32), in_=xh_runs[:].bitcast(I32))
+            for e in range(2):
+                nc.sync.dma_start(out=xh_s[2 + e : P : 32, :].bitcast(I32), in_=xh_runs[16 + e : P : 32, :].bitcast(I32))
+            deal_columns(nc, w2[:].bitcast(I32), w_raw[:].bitcast(I32))
+            deal_columns(nc, w23s[:], ws_raw[:])
+
+        h_bank = [psum.tile([P, S], F32, name="h%d" % t) for t in range(PACK)]
+        h = [sb("h_sb%d" % t, [P, S], F32) for t in range(PACK)]
+        entries = MEMBERS * CHUNK
+        members = [sb("members%d" % c, [P, PACK, entries], F32) for c in range(CHUNKS)]
+        pairs = [sb("pairs%d" % c, [P, PACK, entries // 2], F32) for c in range(CHUNKS)]
+        den = [sb("den%d" % c, [P, PACK, CHUNK], F32) for c in range(CHUNKS)]
+        root = [sb("root%d" % c, [P, PACK, CHUNK], F32) for c in range(CHUNKS)]
+        half = [sb("half%d" % c, [P, PACK, CHUNK], F32) for c in range(CHUNKS)]
+        zi = [sb("zi%d" % c, [P, CHUNK, PACK], BF16) for c in range(CHUNKS)]
+        z_w = [sb("z_w%d" % c, [P, CHUNK], U32) for c in range(CHUNKS)]
+        z_s = [sb("z_s%d" % c, [P, CHUNK], U8) for c in range(CHUNKS)]
+
+        def gather_members(c):
+            window_offsets = n1_sb[:, c * entries // PER_COL : (c + 1) * entries // PER_COL]
+            for t in range(PACK):
+                picked = ex[t][:].indirect(window_offsets)
+                if t in VECTOR_TILES[c]:
+                    nc.vector.tensor_copy(out=members[c][:, t, :], in_=picked)
+                else:
+                    nc.scalar.activation(out=members[c][:, t, :], in_=picked, func=ACT.Copy)
+
+        def add_members(c, tiles):
+            flat = members[c][:, tiles, :].rearrange("p t (k two) -> p (t k) two", two=2)
+            both = pairs[c][:, tiles, :].rearrange("p t (k two) -> p (t k) two", two=2)
+            total = den[c][:, tiles, :].rearrange("p t j -> p (t j)")
+            nc.vector.tensor_tensor(
+                out=pairs[c][:, tiles, :].rearrange("p t k -> p (t k)"), in0=flat[:, :, 0], in1=flat[:, :, 1], op=ALU.add
+            )
+            nc.vector.scalar_tensor_tensor(out=total, in0=both[:, :, 0], scalar=0.5, in1=both[:, :, 1], op0=ALU.add, op1=ALU.add)
+            nc.scalar.activation(
+                out=root[c][:, tiles, :].rearrange("p t j -> p (t j)"), in_=total, func=ACT.Abs_reciprocal_sqrt, scale=0.25
+            )
+
+        def make_z(c):
+            cols = slice(c * CHUNK, (c + 1) * CHUNK)
+            for t in range(PACK):
+                nc.vector.scalar_tensor_tensor(
+                    out=half[c][:, t, :], in0=ex[t][:, cols], scalar=gn_sb[:, t : t + 1], in1=root[c][:, t, :],
+                    op0=ALU.mult, op1=ALU.mult,
+                )
+            nc.vector.tensor_tensor(
+                out=zi[c][:].rearrange("p (g i) t -> p g t i", i=RUN),
+                in0=half[c][:].rearrange("p t (g i) -> p g t i", i=RUN),
+                in1=root[c][:].rearrange("p t (g i) -> p g t i", i=RUN),
+                op=ALU.mult,
+            )
+            nc.vector.quantize_mx(out=z_w[c][:].bitcast(FP8X4), scales=z_s[c][:], in_=zi[c][:].rearrange("p j t -> p (j t)"))
+            for t in range(PACK):
+                rows = slice(t * P, (t + 1) * P)
+                nc.tensor.matmul_mx(
+                    out=h_bank[t][:, cols], lhsT=w3[:, rows].bitcast(FP8X4), lhsT_scale=w23s[4:P, rows],
+                    rhs=xh_w[:, cols].bitcast(FP8X4), rhs_scale=xh_s[:, cols], start=True, stop=False,
+                )
+                nc.tensor.matmul_mx(
+                    out=h_bank[t][:, cols], lhsT=w2[:, rows].bitcast(FP8X4), lhsT_scale=w23s[8:P, rows],
+                    rhs=z_w[c][:].bitcast(FP8X4), rhs_scale=z_s[c][:], start=False, stop=True,
+                )
+
+        early = (CHUNKS - 1) * CHUNK
+        gather_members(0)
+        for c in range(CHUNKS):
+            if c + 1 < CHUNKS:
+                gather_members(c + 1)
+            if c + 1 < CHUNKS:
+                add_members(c, slice(0, PACK))
+            else:
+                add_members(c, slice(0, PACK - 1))
+            if c == 0:
+                prepare_second_layer()
+            if c == CHUNKS - 1:
+                make_z(c - 1)
+                add_members(c, slice(PACK - 1, PACK))
+                for t in range(PACK):
+                    nc.scalar.copy(out=h[t][:, :early], in_=h_bank[t][:, :early])
+            elif c > 0:
+                make_z(c - 1)
+        make_z(CHUNKS - 1)
+        for t in range(PACK):
+            if t == 0:
+                nc.scalar.copy(out=h[t][:, early:], in_=h_bank[t][:, early:])
+            else:
+                nc.vector.tensor_copy(out=h[t][:, early:], in_=h_bank[t][:, early:])
+
+        out_rows = out_0.rearrange("(p t) j -> p t j", t=PACK)
+        out_words = words_of(out_1)
+        o_s = sb("o_s", [P, S], U8)
+        for c, width in enumerate(OUT_CHUNKS):
+            first = sum(OUT_CHUNKS[:c])
+            cols = slice(first, first + width)
+            lists = slice(first // PER_COL, (first + width) // PER_COL)
+            less = sb("less%d" % c, [P, PACK, width], F32)
+            gap = sb("gap%d" % c, [P, PACK, width], F32)
+            gap_i = sb("gap_i%d" % c, [P, width, PACK], BF16)
+            o_w = sb("o_w%d" % c, [P, width], U32)
+            for t in range(PACK):
+                nc.scalar.activation(out=less[:, t, :], in_=h[t][:].indirect(n3_sb[:, lists]), func=ACT.Copy)
+                nc.vector.tensor_tensor(out=gap[:, t, :], in0=h[t][:].indirect(n2_sb[:, lists]), in1=less[:, t, :], op=ALU.subtract)
+            nc.sync.dma_start(out=out_rows[:, :, cols], in_=gap[:])
+            woven = gap_i[:].rearrange("p (g i) t -> p g t i", i=RUN)
+            source = gap[:].rearrange("p t (g i) -> p g t i", i=RUN)
+            if c == 0:
+                nc.scalar.copy(out=woven, in_=source)
+            else:
+                nc.vector.tensor_copy(out=woven, in_=source)
+            nc.vector.quantize_mx(out=o_w[:].bitcast(FP8X4), scales=o_s[:, cols], in_=gap_i[:].rearrange("p j t -> p (j t)"))
+            nc.sync.dma_start(out=out_words[:, cols], in_=o_w[:].bitcast(I32))
+        scale_rows = out_2[0].bitcast(I32)
+        for q in range(4):
+            queue = nc.sync if q % 2 == 0 else nc.scalar
+            queue.dma_start(out=scale_rows[4 * q : 4 * q + 4, :], in_=o_s[32 * q : 32 * q + 4, :].bitcast(I32))

@@ -1,6 +1,7 @@
 from contextlib import ExitStack
 
 import concourse.mybir as mybir
+from concourse.masks import make_identity
 
 K, T, S, H, N = 512, 2048, 512, 512, 512
 FLOPS = 3 * 2 * 512 * 512 * 512
@@ -19,12 +20,16 @@ P = 128
 PACK = 4
 MEMBERS = 4
 PER_COL = 16
-SPARE = 32
+SPARE = 192
 CHUNK = 128
 CHUNKS = S // CHUNK
-VECTOR_TILES = ((0, 1, 2), (0, 1), (), ())
+VECTOR_SHARE = (2, 2, 2, 2)
+RING = 9
+FIRST_SQUARED = 2
+HALF = S // 2
 OUT_CHUNKS = (256, 128, 128)
 RUN = 4
+SCALAR_WEAVES = (0,)
 
 
 def words_of(dram_words):
@@ -50,8 +55,8 @@ def tile_picked_mixhgsharegap_none_po_kernel(
         keep = ctx.enter_context(tc.tile_pool(name="keep", bufs=1))
         psum = ctx.enter_context(tc.psum_pool(name="psum", bufs=1))
 
-        def sb(name, shape, dtype):
-            return keep.tile(shape, dtype, name=name, align_bytes=64)
+        def sb(name, shape, dtype, tag=None):
+            return keep.tile(shape, dtype, name=name, tag=tag or name, align_bytes=64)
 
         offs_sb = sb("offs_sb", [P, S // PER_COL], U16)
         hz_sb = sb("hz_sb", [P, S // PER_COL], U16)
@@ -60,174 +65,243 @@ def tile_picked_mixhgsharegap_none_po_kernel(
         n3_sb = sb("n3_sb", [P, S // PER_COL], U16)
         xw = sb("xw", [P, T], U32)
         xs = sb("xs", [P, T], U8)
-        xs_runs = sb("xs_runs", [P, T], U8)
-        w_raw = sb("w_raw", [P, H], U32)
-        ws_raw = sb("ws_raw", [P, H], U8)
+        w1_raw = sb("w1_raw", [P, H], U32)
+        w2_raw = sb("w2_raw", [P, N], U32)
+        w3_raw = sb("w3_raw", [P, N], U32)
+        w1s_raw = sb("w1s_raw", [P, H], U8)
+        w23s_raw = sb("w23s_raw", [P, N], U8)
+        xh_s = sb("xh_s", [P, S], U8)
         gn_sb = sb("gn_sb", [P, PACK], F32)
         zeros = sb("zeros", [P, SPARE], F32)
+        ident = sb("ident", [P, P], F32)
 
-        nc.gpsimd.memset(xs[:].bitcast(I32), 0)
-        nc.gpsimd.memset(ws_raw[:].bitcast(I32), 0)
-        nc.gpsimd.memset(zeros[:], 0.0)
+        nc.vector.memset(xs[:].bitcast(I32), 0)
+        nc.vector.memset(zeros[:], 0.0)
+        nc.gpsimd.memset(w1s_raw[:].bitcast(I32), 0)
+        nc.gpsimd.memset(w23s_raw[:].bitcast(I32), 0)
+        nc.gpsimd.memset(xh_s[:].bitcast(I32), 0)
+        make_identity(nc, ident[:])
 
-        for tile, dram in ((offs_sb, offs), (hz_sb, hz), (n1_sb, n1), (n3_sb, n3), (n2_sb, n2)):
-            nc.sync.dma_start(tile[:], dram)
-        nc.sync.dma_start(out=w_raw[:].bitcast(I32), in_=words_of(w1_words))
-        nc.sync.dma_start(out=xw[:].bitcast(I32), in_=words_of(x_words))
-        load_scale_rows([nc.scalar] * 4, xs, 0, x_scales)
-        load_scale_rows([nc.scalar] * 3 + [nc.gpsimd], ws_raw, 0, w1_scales)
-        nc.gpsimd.memset(xs_runs[:].bitcast(I32), 0)
-        nc.scalar.dma_start(out=gn_sb[:], in_=gn.rearrange("(p t) o -> p (t o)", t=PACK))
         x_rows = x_scales[0].bitcast(I32)
+        nc.sync.dma_start(offs_sb[:], offs)
+        nc.sync.dma_start(hz_sb[:], hz)
+        nc.sync.dma_start(out=w1_raw[:].bitcast(I32), in_=words_of(w1_words))
         for e in range(2):
-            nc.sync.dma_start(out=xs_runs[e:P:16, :].bitcast(I32), in_=x_rows[e:16:2, :])
+            nc.scalar.dma_start(out=xs[e:P:16, :].bitcast(I32), in_=x_rows[e:16:2, :])
+        for e in range(2):
+            nc.sync.dma_start(out=xs[2 + e : P : 32, :].bitcast(I32), in_=x_rows[2 + e : 16 : 4, :])
+        nc.sync.dma_start(out=xw[:].bitcast(I32), in_=words_of(x_words))
+        load_scale_rows((nc.sync,) * 4, w1s_raw, 0, w1_scales)
+        nc.sync.dma_start(n1_sb[:], n1)
+        nc.sync.dma_start(out=w3_raw[:].bitcast(I32), in_=words_of(w3_words))
+        nc.sync.dma_start(out=w2_raw[:].bitcast(I32), in_=words_of(w2_words))
+        load_scale_rows((nc.sync,) * 4, w23s_raw, 0, w3_scales)
+        load_scale_rows((nc.sync,) * 4, w23s_raw, 4, w2_scales)
+        nc.sync.dma_start(out=gn_sb[:], in_=gn.rearrange("(p t) o -> p (t o)", t=PACK))
+        nc.sync.dma_start(n3_sb[:], n3)
+        nc.sync.dma_start(n2_sb[:], n2)
 
         ex = [sb("ex%d" % t, [P, S + SPARE], F32) for t in range(PACK)]
         for t in range(PACK):
             nc.scalar.activation(out=ex[t][:, S:], in_=zeros[:], func=ACT.Copy)
 
+        y_half = {}
         xq_s = sb("xq_s", [P, S], U8)
-        xq_w = sb("xq_w", [P, S], U32)
+        first_w = sb("first_w", [P, HALF], U32)
+        later_w = sb("later_w", [P, HALF + S], U32, tag="w1s_raw")
+        xq_w = (first_w[:], later_w[:, :HALF])
+        xh_w = later_w[:, HALF:]
+        xh_runs = sb("xh_runs", [P, S], U8)
         w1 = sb("w1", [P, H], U32)
         w1s = sb("w1s", [P, H], U8)
-        nc.vector.tensor_copy(out=xq_s[:], in_=xs[:].indirect(offs_sb[:]))
-        deal_columns(nc, w1[:].bitcast(I32), w_raw[:].bitcast(I32))
-        nc.vector.tensor_copy(out=xq_w[:], in_=xw[:].indirect(offs_sb[:]))
-        deal_columns(nc, w1s[:], ws_raw[:])
-        nc.sync.dma_start(out=w_raw[:].bitcast(I32), in_=words_of(w3_words))
-        load_scale_rows([nc.sync] * 4, ws_raw, 4, w3_scales)
-        load_scale_rows([nc.sync] * 4, ws_raw, 8, w2_scales)
-
-        for t in range(PACK):
-            cols = slice(t * P, (t + 1) * P)
-            y = psum.tile([P, S], F32, name="y%d" % t)
-            nc.tensor.matmul_mx(
-                out=y[:], lhsT=w1[:, cols].bitcast(FP8X4), lhsT_scale=w1s[:, cols],
-                rhs=xq_w[:].bitcast(FP8X4), rhs_scale=xq_s[:], start=True, stop=True,
-            )
-            nc.scalar.activation(out=ex[t][:, :S], in_=y[:], func=ACT.Exp, scale=0.5)
-
-        xh_w = sb("xh_w", [P, S], U32)
-        xh_runs = sb("xh_runs", [P, S], U8)
-        xh_s = sb("xh_s", [P, S], U8)
-        nc.vector.tensor_copy(out=xh_w[:], in_=xw[:].indirect(hz_sb[:]))
-
         w2 = sb("w2", [P, N], U32)
         w3 = sb("w3", [P, N], U32)
         w23s = sb("w23s", [P, N], U8)
 
-        deal_columns(nc, w3[:].bitcast(I32), w_raw[:].bitcast(I32))
-        nc.sync.dma_start(out=w_raw[:].bitcast(I32), in_=words_of(w2_words))
+        nc.vector.tensor_copy(out=xq_s[:], in_=xs[:].indirect(offs_sb[:]))
+        deal_columns(nc, w1[:].bitcast(I32), w1_raw[:].bitcast(I32))
+        nc.vector.tensor_copy(out=xh_runs[:], in_=xs[:].indirect(hz_sb[:]))
+        for u in range(2):
+            cols = slice(u * HALF, (u + 1) * HALF)
+            nc.vector.tensor_copy(out=xq_w[u], in_=xw[:].indirect(offs_sb[:, u * HALF // PER_COL : (u + 1) * HALF // PER_COL]))
+            if u == 0:
+                deal_columns(nc, w1s[:], w1s_raw[:])
+            for pair in range(2):
+                y = psum.tile([P, 2, HALF], F32, name="y%d_%d" % (u, pair), tag="bank%d" % (2 * u + pair))
+                for e in range(2):
+                    rows = slice((2 * pair + e) * P, (2 * pair + e + 1) * P)
+                    nc.tensor.matmul_mx(
+                        out=y[:, e, :], lhsT=w1[:, rows].bitcast(FP8X4), lhsT_scale=w1s[:, rows],
+                        rhs=xq_w[u].bitcast(FP8X4), rhs_scale=xq_s[:, cols], start=True, stop=True,
+                    )
+                y_half.setdefault((u, pair), y)
+        for pair in range(2):
+            for u in range(2):
+                for e in range(2):
+                    nc.scalar.activation(
+                        out=ex[2 * pair + e][:, u * HALF : (u + 1) * HALF], in_=y_half[u, pair][:, e, :], func=ACT.Exp, scale=0.5
+                    )
+        nc.vector.tensor_copy(out=xh_w, in_=xw[:].indirect(hz_sb[:]))
+        for e in range(2):
+            nc.sync.dma_start(out=xh_s[e:P:32, :].bitcast(I32), in_=xh_runs[e:P:32, :].bitcast(I32))
+            nc.sync.dma_start(out=xh_s[2 + e : P : 32, :].bitcast(I32), in_=xh_runs[16 + e : P : 32, :].bitcast(I32))
 
-        def prepare_second_layer():
-            nc.vector.tensor_copy(out=xh_runs[:], in_=xs_runs[:].indirect(hz_sb[:]))
-            nc.vector.tensor_copy(out=xh_s[:].bitcast(I32), in_=xh_runs[:].bitcast(I32))
-            for e in range(2):
-                nc.sync.dma_start(out=xh_s[2 + e : P : 32, :].bitcast(I32), in_=xh_runs[16 + e : P : 32, :].bitcast(I32))
-            deal_columns(nc, w2[:].bitcast(I32), w_raw[:].bitcast(I32))
-            deal_columns(nc, w23s[:], ws_raw[:])
-
-        h_bank = [psum.tile([P, S], F32, name="h%d" % t) for t in range(PACK)]
-        h = [sb("h_sb%d" % t, [P, S], F32) for t in range(PACK)]
+        h = []
         entries = MEMBERS * CHUNK
-        members = [sb("members%d" % c, [P, PACK, entries], F32) for c in range(CHUNKS)]
-        pairs = [sb("pairs%d" % c, [P, PACK, entries // 2], F32) for c in range(CHUNKS)]
-        den = [sb("den%d" % c, [P, PACK, CHUNK], F32) for c in range(CHUNKS)]
-        root = [sb("root%d" % c, [P, PACK, CHUNK], F32) for c in range(CHUNKS)]
+        last = CHUNKS - 1
+        members = {}
+        pair_sums = sb("pair_sums", [P, PACK, CHUNK, 2], F32)
+        pairs = pair_sums[:].rearrange("p t j m -> p t m j")
+        ring = []
+        root_t = [sb("root_t%d" % c, [P, PACK, P], F32) for c in range(last)]
+        den = sb("den", [P, PACK, CHUNK], F32)
+        root = {last: sb("root_last", [P, PACK, CHUNK], F32)}
         half = [sb("half%d" % c, [P, PACK, CHUNK], F32) for c in range(CHUNKS)]
         zi = [sb("zi%d" % c, [P, CHUNK, PACK], BF16) for c in range(CHUNKS)]
         z_w = [sb("z_w%d" % c, [P, CHUNK], U32) for c in range(CHUNKS)]
         z_s = [sb("z_s%d" % c, [P, CHUNK], U8) for c in range(CHUNKS)]
+        h_bank = {}
+        share_t = {c: sb("share%d" % c, [P, PACK, CHUNK], F32) for c in range(FIRST_SQUARED, CHUNKS)}
 
         def gather_members(c):
             window_offsets = n1_sb[:, c * entries // PER_COL : (c + 1) * entries // PER_COL]
             for t in range(PACK):
-                picked = ex[t][:].indirect(window_offsets)
-                if t in VECTOR_TILES[c]:
-                    nc.vector.tensor_copy(out=members[c][:, t, :], in_=picked)
+                if t < VECTOR_SHARE[c]:
+                    unit = sb("members%d_%d" % (c, t), [P, MEMBERS, CHUNK], F32)
+                    nc.vector.tensor_copy(
+                        out=unit[:].bitcast(U32).rearrange("p m j -> p j m"), in_=ex[t][:].bitcast(U32).indirect(window_offsets)
+                    )
+                    members.setdefault((c, t), unit[:])
                 else:
-                    nc.scalar.activation(out=members[c][:, t, :], in_=picked, func=ACT.Copy)
+                    unit = sb("members%d_%d" % (c, t), [P, entries], F32, tag="ring%d" % (len(ring) % RING))
+                    ring.append(unit)
+                    nc.scalar.activation(out=unit[:], in_=ex[t][:].indirect(window_offsets), func=ACT.Copy)
+                    members.setdefault((c, t), unit[:].rearrange("p (j m) -> p m j", m=MEMBERS))
 
-        def add_members(c, tiles):
-            flat = members[c][:, tiles, :].rearrange("p t (k two) -> p (t k) two", two=2)
-            both = pairs[c][:, tiles, :].rearrange("p t (k two) -> p (t k) two", two=2)
-            total = den[c][:, tiles, :].rearrange("p t j -> p (t j)")
-            nc.vector.tensor_tensor(
-                out=pairs[c][:, tiles, :].rearrange("p t k -> p (t k)"), in0=flat[:, :, 0], in1=flat[:, :, 1], op=ALU.add
-            )
-            nc.vector.scalar_tensor_tensor(out=total, in0=both[:, :, 0], scalar=0.5, in1=both[:, :, 1], op0=ALU.add, op1=ALU.add)
-            nc.scalar.activation(
-                out=root[c][:, tiles, :].rearrange("p t j -> p (t j)"), in_=total, func=ACT.Abs_reciprocal_sqrt, scale=0.25
-            )
-
-        def make_z(c):
-            cols = slice(c * CHUNK, (c + 1) * CHUNK)
+        def roots_by_transposes(c):
+            total = psum.tile([P, PACK, P], F32, name="total%d" % c, tag="bank%d" % (c % 2))
             for t in range(PACK):
+                for m in range(MEMBERS):
+                    nc.tensor.matmul(
+                        total[:, t, :], lhsT=members[c, t][:, m, :], rhs=ident[:],
+                        start=m == 0, stop=m == MEMBERS - 1, is_transpose=True,
+                    )
+            nc.scalar.activation(out=root_t[c][:], in_=total[:], func=ACT.Abs_reciprocal_sqrt, scale=0.25, bias=0.125)
+            turned = root_t[c]
+            if c >= FIRST_SQUARED:
+                turned = share_t[c]
+                nc.scalar.activation(out=turned[:], in_=root_t[c][:], func=ACT.Square)
+            root.setdefault(c, psum.tile([P, PACK, CHUNK], F32, name="root%d" % c, tag="bank%d" % (2 + c % 2)))
+            for t in range(PACK):
+                nc.tensor.transpose(root[c][:, t, :], turned[:, t, :], ident[:])
+
+        def roots_in_place(c, tiles):
+            for t in range(tiles.start, tiles.stop):
+                nc.vector.tensor_tensor(
+                    out=pairs[:, t, :, :].rearrange("p m j -> p j m"),
+                    in0=members[c, t][:, 0:2, :].rearrange("p m j -> p j m"),
+                    in1=members[c, t][:, 2:4, :].rearrange("p m j -> p j m"), op=ALU.add,
+                )
+            nc.vector.tensor_tensor(out=den[:, tiles, :], in0=pairs[:, tiles, 0, :], in1=pairs[:, tiles, 1, :], op=ALU.add)
+            nc.scalar.activation(out=root[c][:, tiles, :], in_=den[:, tiles, :], func=ACT.Abs_reciprocal_sqrt, scale=0.25, bias=0.125)
+            if c >= FIRST_SQUARED:
+                nc.scalar.activation(out=share_t[c][:, tiles, :], in_=root[c][:, tiles, :], func=ACT.Square)
+
+        def h_slot(c, t):
+            return h_bank[c, min(t, 1) if c == last else 0][:, t, :]
+
+        def open_h(c):
+            cols = slice(c * CHUNK, (c + 1) * CHUNK)
+            if c == last:
+                h_bank.setdefault((c, 0), psum.tile([P, PACK, CHUNK], F32, name="h_last0"))
+                h_bank.setdefault((c, 1), psum.tile([P, PACK, CHUNK], F32, name="h_last1", tag="bank1"))
+            else:
+                h_bank.setdefault((c, 0), psum.tile([P, PACK, CHUNK], F32, name="h%d" % c))
+            for t in range(PACK):
+                rows = slice(t * P, (t + 1) * P)
+                nc.tensor.matmul_mx(
+                    out=h_slot(c, t), lhsT=w3[:, rows].bitcast(FP8X4), lhsT_scale=w23s[:, rows],
+                    rhs=xh_w[:, cols].bitcast(FP8X4), rhs_scale=xh_s[:, cols], start=t == 0 or (c == last and t == 1), stop=False,
+                )
+
+        def scale_tiles(c, tiles):
+            cols = slice(c * CHUNK, (c + 1) * CHUNK)
+            for t in range(tiles.start, tiles.stop):
+                if c >= FIRST_SQUARED:
+                    nc.scalar.activation(out=half[c][:, t, :], in_=ex[t][:, cols], func=ACT.Copy, scale=gn_sb[:, t : t + 1])
+                    continue
                 nc.vector.scalar_tensor_tensor(
                     out=half[c][:, t, :], in0=ex[t][:, cols], scalar=gn_sb[:, t : t + 1], in1=root[c][:, t, :],
                     op0=ALU.mult, op1=ALU.mult,
                 )
+
+        def make_z(c):
             nc.vector.tensor_tensor(
                 out=zi[c][:].rearrange("p (g i) t -> p g t i", i=RUN),
                 in0=half[c][:].rearrange("p t (g i) -> p g t i", i=RUN),
-                in1=root[c][:].rearrange("p t (g i) -> p g t i", i=RUN),
+                in1=(share_t[c] if c == last and c >= FIRST_SQUARED else root[c])[:].rearrange("p t (g i) -> p g t i", i=RUN),
                 op=ALU.mult,
             )
             nc.vector.quantize_mx(out=z_w[c][:].bitcast(FP8X4), scales=z_s[c][:], in_=zi[c][:].rearrange("p j t -> p (j t)"))
             for t in range(PACK):
                 rows = slice(t * P, (t + 1) * P)
                 nc.tensor.matmul_mx(
-                    out=h_bank[t][:, cols], lhsT=w3[:, rows].bitcast(FP8X4), lhsT_scale=w23s[4:P, rows],
-                    rhs=xh_w[:, cols].bitcast(FP8X4), rhs_scale=xh_s[:, cols], start=True, stop=False,
-                )
-                nc.tensor.matmul_mx(
-                    out=h_bank[t][:, cols], lhsT=w2[:, rows].bitcast(FP8X4), lhsT_scale=w23s[8:P, rows],
-                    rhs=z_w[c][:].bitcast(FP8X4), rhs_scale=z_s[c][:], start=False, stop=True,
+                    out=h_slot(c, t), lhsT=w2[:, rows].bitcast(FP8X4), lhsT_scale=w23s[4:P, rows],
+                    rhs=z_w[c][:].bitcast(FP8X4), rhs_scale=z_s[c][:], start=False, stop=t == PACK - 1 or (c == last and t == 0),
                 )
 
-        early = (CHUNKS - 1) * CHUNK
+        def copy_h(c):
+            cols = slice(c * CHUNK, (c + 1) * CHUNK)
+            for t in range(PACK):
+                if c == last and t >= 1:
+                    nc.vector.tensor_copy(out=h[t][:, cols], in_=h_slot(c, t))
+                else:
+                    nc.scalar.copy(out=h[t][:, cols], in_=h_slot(c, t))
+
+        every, most, rest = slice(0, PACK), slice(0, PACK - 1), slice(PACK - 1, PACK)
         gather_members(0)
-        for c in range(CHUNKS):
-            if c + 1 < CHUNKS:
-                gather_members(c + 1)
-            if c + 1 < CHUNKS:
-                add_members(c, slice(0, PACK))
-            else:
-                add_members(c, slice(0, PACK - 1))
-            if c == 0:
-                prepare_second_layer()
-            if c == CHUNKS - 1:
-                make_z(c - 1)
-                add_members(c, slice(PACK - 1, PACK))
-                for t in range(PACK):
-                    nc.scalar.copy(out=h[t][:, :early], in_=h_bank[t][:, :early])
-            elif c > 0:
-                make_z(c - 1)
-        make_z(CHUNKS - 1)
-        for t in range(PACK):
-            if t == 0:
-                nc.scalar.copy(out=h[t][:, early:], in_=h_bank[t][:, early:])
-            else:
-                nc.vector.tensor_copy(out=h[t][:, early:], in_=h_bank[t][:, early:])
+        gather_members(1)
+        deal_columns(nc, w3[:].bitcast(I32), w3_raw[:].bitcast(I32))
+        deal_columns(nc, w23s[:], w23s_raw[:])
+        deal_columns(nc, w2[:].bitcast(I32), w2_raw[:].bitcast(I32))
+        for c in range(last):
+            roots_by_transposes(c)
+            open_h(c)
+            if c + 2 < CHUNKS:
+                gather_members(c + 2)
+            scale_tiles(c, every)
+            make_z(c)
+        open_h(last)
+        h.extend([sb("h_sb%d" % t, [P, S], F32) for t in range(PACK)])
+        roots_in_place(last, most)
+        roots_in_place(last, rest)
+        scale_tiles(last, every)
+        for c in range(last):
+            copy_h(c)
+        make_z(last)
+        copy_h(last)
 
         out_rows = out_0.rearrange("(p t) j -> p t j", t=PACK)
         out_words = words_of(out_1)
         o_s = sb("o_s", [P, S], U8)
+        gaps = []
         for c, width in enumerate(OUT_CHUNKS):
             first = sum(OUT_CHUNKS[:c])
             cols = slice(first, first + width)
             lists = slice(first // PER_COL, (first + width) // PER_COL)
             less = sb("less%d" % c, [P, PACK, width], F32)
             gap = sb("gap%d" % c, [P, PACK, width], F32)
-            gap_i = sb("gap_i%d" % c, [P, width, PACK], BF16)
-            o_w = sb("o_w%d" % c, [P, width], U32)
             for t in range(PACK):
                 nc.scalar.activation(out=less[:, t, :], in_=h[t][:].indirect(n3_sb[:, lists]), func=ACT.Copy)
                 nc.vector.tensor_tensor(out=gap[:, t, :], in0=h[t][:].indirect(n2_sb[:, lists]), in1=less[:, t, :], op=ALU.subtract)
             nc.sync.dma_start(out=out_rows[:, :, cols], in_=gap[:])
+            gaps.append((cols, width, gap))
+        for c, (cols, width, gap) in enumerate(gaps):
+            gap_i = sb("gap_i%d" % c, [P, width, PACK], BF16)
+            o_w = sb("o_w%d" % c, [P, width], U32)
             woven = gap_i[:].rearrange("p (g i) t -> p g t i", i=RUN)
             source = gap[:].rearrange("p t (g i) -> p g t i", i=RUN)
-            if c == 0:
+            if c in SCALAR_WEAVES:
                 nc.scalar.copy(out=woven, in_=source)
             else:
                 nc.vector.tensor_copy(out=woven, in_=source)

@@ -20,14 +20,15 @@ P = 128
 PACK = 4
 MEMBERS = 4
 PER_COL = 16
-SPARE = 192
+SPARE = 193
 CHUNK = 128
 CHUNKS = S // CHUNK
-VECTOR_SHARE = (2, 2, 2, 2)
+VECTOR_SHARE = (2, 3, 2, 1)
 RING = 9
 FIRST_SQUARED = 2
 HALF = S // 2
 OUT_CHUNKS = (256, 128, 128)
+LATE = 2
 RUN = 4
 SCALAR_WEAVES = (0,)
 
@@ -42,8 +43,8 @@ def load_scale_rows(queues, plane, first, dram_scales):
         queues[q].dma_start(out=plane[32 * q + first : 32 * q + first + 4, :].bitcast(I32), in_=rows[4 * q : 4 * q + 4, :])
 
 
-def deal_columns(nc, dealt, raw):
-    nc.vector.tensor_copy(out=dealt.rearrange("p (t m) -> p t m", t=PACK), in_=raw.rearrange("p (m t) -> p t m", t=PACK))
+def deal_columns(engine, dealt, raw):
+    engine.tensor_copy(out=dealt.rearrange("p (t m) -> p t m", t=PACK), in_=raw.rearrange("p (m t) -> p t m", t=PACK))
 
 
 def tile_picked_mixhgsharegap_none_po_kernel(
@@ -84,7 +85,6 @@ def tile_picked_mixhgsharegap_none_po_kernel(
 
         x_rows = x_scales[0].bitcast(I32)
         nc.sync.dma_start(offs_sb[:], offs)
-        nc.sync.dma_start(hz_sb[:], hz)
         nc.sync.dma_start(out=w1_raw[:].bitcast(I32), in_=words_of(w1_words))
         for e in range(2):
             nc.scalar.dma_start(out=xs[e:P:16, :].bitcast(I32), in_=x_rows[e:16:2, :])
@@ -92,6 +92,7 @@ def tile_picked_mixhgsharegap_none_po_kernel(
             nc.sync.dma_start(out=xs[2 + e : P : 32, :].bitcast(I32), in_=x_rows[2 + e : 16 : 4, :])
         nc.sync.dma_start(out=xw[:].bitcast(I32), in_=words_of(x_words))
         load_scale_rows((nc.sync,) * 4, w1s_raw, 0, w1_scales)
+        nc.sync.dma_start(hz_sb[:], hz)
         nc.sync.dma_start(n1_sb[:], n1)
         nc.sync.dma_start(out=w3_raw[:].bitcast(I32), in_=words_of(w3_words))
         nc.sync.dma_start(out=w2_raw[:].bitcast(I32), in_=words_of(w2_words))
@@ -111,21 +112,18 @@ def tile_picked_mixhgsharegap_none_po_kernel(
         later_w = sb("later_w", [P, HALF + S], U32, tag="w1s_raw")
         xq_w = (first_w[:], later_w[:, :HALF])
         xh_w = later_w[:, HALF:]
-        xh_runs = sb("xh_runs", [P, S], U8)
+        xh_runs = sb("xh_runs", [P, S], U8, tag="first_w")
         w1 = sb("w1", [P, H], U32)
         w1s = sb("w1s", [P, H], U8)
-        w2 = sb("w2", [P, N], U32)
-        w3 = sb("w3", [P, N], U32)
         w23s = sb("w23s", [P, N], U8)
 
         nc.vector.tensor_copy(out=xq_s[:], in_=xs[:].indirect(offs_sb[:]))
-        deal_columns(nc, w1[:].bitcast(I32), w1_raw[:].bitcast(I32))
-        nc.vector.tensor_copy(out=xh_runs[:], in_=xs[:].indirect(hz_sb[:]))
+        deal_columns(nc.vector, w1[:].bitcast(I32), w1_raw[:].bitcast(I32))
         for u in range(2):
             cols = slice(u * HALF, (u + 1) * HALF)
             nc.vector.tensor_copy(out=xq_w[u], in_=xw[:].indirect(offs_sb[:, u * HALF // PER_COL : (u + 1) * HALF // PER_COL]))
             if u == 0:
-                deal_columns(nc, w1s[:], w1s_raw[:])
+                deal_columns(nc.vector, w1s[:], w1s_raw[:])
             for pair in range(2):
                 y = psum.tile([P, 2, HALF], F32, name="y%d_%d" % (u, pair), tag="bank%d" % (2 * u + pair))
                 for e in range(2):
@@ -142,10 +140,13 @@ def tile_picked_mixhgsharegap_none_po_kernel(
                         out=ex[2 * pair + e][:, u * HALF : (u + 1) * HALF], in_=y_half[u, pair][:, e, :], func=ACT.Exp, scale=0.5
                     )
         nc.vector.tensor_copy(out=xh_w, in_=xw[:].indirect(hz_sb[:]))
+        nc.vector.tensor_copy(out=xh_runs[:], in_=xs[:].indirect(hz_sb[:]))
         for e in range(2):
             nc.sync.dma_start(out=xh_s[e:P:32, :].bitcast(I32), in_=xh_runs[e:P:32, :].bitcast(I32))
             nc.sync.dma_start(out=xh_s[2 + e : P : 32, :].bitcast(I32), in_=xh_runs[16 + e : P : 32, :].bitcast(I32))
 
+        w23 = sb("w23", [P, 2 * N], U32, tag="xq_s")
+        w3, w2 = w23[:, :N], w23[:, N:]
         h = []
         entries = MEMBERS * CHUNK
         last = CHUNKS - 1
@@ -161,6 +162,7 @@ def tile_picked_mixhgsharegap_none_po_kernel(
         z_w = [sb("z_w%d" % c, [P, CHUNK], U32) for c in range(CHUNKS)]
         z_s = [sb("z_s%d" % c, [P, CHUNK], U8) for c in range(CHUNKS)]
         h_bank = {}
+        gained = sb("gained", [P, PACK, S - FIRST_SQUARED * CHUNK], F32)
         share_t = {c: sb("share%d" % c, [P, PACK, CHUNK], F32) for c in range(FIRST_SQUARED, CHUNKS)}
 
         def gather_members(c):
@@ -207,38 +209,46 @@ def tile_picked_mixhgsharegap_none_po_kernel(
             if c >= FIRST_SQUARED:
                 nc.scalar.activation(out=share_t[c][:, tiles, :], in_=root[c][:, tiles, :], func=ACT.Square)
 
-        def h_slot(c, t):
-            return h_bank[c, min(t, 1) if c == last else 0][:, t, :]
+        def h_columns(t, cols):
+            if cols.start >= LATE * CHUNK:
+                return h_bank[LATE, min(t, 2)][:, t // 3, cols.start - LATE * CHUNK : cols.stop - LATE * CHUNK]
+            return h_bank[cols.start // CHUNK, 0][:, t, :]
 
         def open_h(c):
-            cols = slice(c * CHUNK, (c + 1) * CHUNK)
-            if c == last:
-                h_bank.setdefault((c, 0), psum.tile([P, PACK, CHUNK], F32, name="h_last0"))
-                h_bank.setdefault((c, 1), psum.tile([P, PACK, CHUNK], F32, name="h_last1", tag="bank1"))
-            else:
+            if c < LATE:
+                cols = slice(c * CHUNK, (c + 1) * CHUNK)
                 h_bank.setdefault((c, 0), psum.tile([P, PACK, CHUNK], F32, name="h%d" % c))
+            else:
+                cols = slice(LATE * CHUNK, S)
+                for b, tag in enumerate(("h_late0", "h_late1", "bank1")):
+                    h_bank.setdefault((c, b), psum.tile([P, 2, S - LATE * CHUNK], F32, name="h_late%d" % b, tag=tag))
             for t in range(PACK):
                 rows = slice(t * P, (t + 1) * P)
                 nc.tensor.matmul_mx(
-                    out=h_slot(c, t), lhsT=w3[:, rows].bitcast(FP8X4), lhsT_scale=w23s[:, rows],
-                    rhs=xh_w[:, cols].bitcast(FP8X4), rhs_scale=xh_s[:, cols], start=t == 0 or (c == last and t == 1), stop=False,
+                    out=h_columns(t, cols), lhsT=w3[:, rows].bitcast(FP8X4), lhsT_scale=w23s[:, rows],
+                    rhs=xh_w[:, cols].bitcast(FP8X4), rhs_scale=xh_s[:, cols], start=t == 0 or (c == LATE and t < 3), stop=False,
                 )
 
         def scale_tiles(c, tiles):
             cols = slice(c * CHUNK, (c + 1) * CHUNK)
             for t in range(tiles.start, tiles.stop):
                 if c >= FIRST_SQUARED:
-                    nc.scalar.activation(out=half[c][:, t, :], in_=ex[t][:, cols], func=ACT.Copy, scale=gn_sb[:, t : t + 1])
                     continue
                 nc.vector.scalar_tensor_tensor(
                     out=half[c][:, t, :], in0=ex[t][:, cols], scalar=gn_sb[:, t : t + 1], in1=root[c][:, t, :],
                     op0=ALU.mult, op1=ALU.mult,
                 )
 
+        def apply_gain():
+            for t in range(PACK):
+                nc.gpsimd.tensor_scalar(
+                    out=gained[:, t, :], in0=ex[t][:, FIRST_SQUARED * CHUNK : S], scalar1=gn_sb[:, t : t + 1], scalar2=0.0, op0=ALU.mult, op1=ALU.add
+                )
+
         def make_z(c):
             nc.vector.tensor_tensor(
                 out=zi[c][:].rearrange("p (g i) t -> p g t i", i=RUN),
-                in0=half[c][:].rearrange("p t (g i) -> p g t i", i=RUN),
+                in0=(half[c][:] if c < FIRST_SQUARED else gained[:, :, (c - FIRST_SQUARED) * CHUNK : (c - FIRST_SQUARED + 1) * CHUNK]).rearrange("p t (g i) -> p g t i", i=RUN),
                 in1=(share_t[c] if c == last and c >= FIRST_SQUARED else root[c])[:].rearrange("p t (g i) -> p g t i", i=RUN),
                 op=ALU.mult,
             )
@@ -246,40 +256,41 @@ def tile_picked_mixhgsharegap_none_po_kernel(
             for t in range(PACK):
                 rows = slice(t * P, (t + 1) * P)
                 nc.tensor.matmul_mx(
-                    out=h_slot(c, t), lhsT=w2[:, rows].bitcast(FP8X4), lhsT_scale=w23s[4:P, rows],
-                    rhs=z_w[c][:].bitcast(FP8X4), rhs_scale=z_s[c][:], start=False, stop=t == PACK - 1 or (c == last and t == 0),
+                    out=h_columns(t, slice(c * CHUNK, (c + 1) * CHUNK)), lhsT=w2[:, rows].bitcast(FP8X4), lhsT_scale=w23s[4:P, rows],
+                    rhs=z_w[c][:].bitcast(FP8X4), rhs_scale=z_s[c][:], start=False, stop=(t != 2 if c == last else c < LATE and t == PACK - 1),
                 )
 
         def copy_h(c):
-            cols = slice(c * CHUNK, (c + 1) * CHUNK)
+            cols = slice(c * CHUNK, (c + 1) * CHUNK if c < LATE else S)
             for t in range(PACK):
-                if c == last and t >= 1:
-                    nc.vector.tensor_copy(out=h[t][:, cols], in_=h_slot(c, t))
+                if c == LATE and t >= 1:
+                    nc.vector.tensor_copy(out=h[t][:, cols], in_=h_columns(t, cols))
                 else:
-                    nc.scalar.copy(out=h[t][:, cols], in_=h_slot(c, t))
+                    nc.scalar.copy(out=h[t][:, cols], in_=h_columns(t, cols))
 
         every, most, rest = slice(0, PACK), slice(0, PACK - 1), slice(PACK - 1, PACK)
         gather_members(0)
         gather_members(1)
-        deal_columns(nc, w3[:].bitcast(I32), w3_raw[:].bitcast(I32))
-        deal_columns(nc, w23s[:], w23s_raw[:])
-        deal_columns(nc, w2[:].bitcast(I32), w2_raw[:].bitcast(I32))
+        deal_columns(nc.gpsimd, w3.bitcast(I32), w3_raw[:].bitcast(I32))
+        deal_columns(nc.gpsimd, w23s[:], w23s_raw[:])
+        deal_columns(nc.gpsimd, w2.bitcast(I32), w2_raw[:].bitcast(I32))
         for c in range(last):
             roots_by_transposes(c)
             open_h(c)
             if c + 2 < CHUNKS:
                 gather_members(c + 2)
             scale_tiles(c, every)
+            if c == 0:
+                apply_gain()
             make_z(c)
-        open_h(last)
         h.extend([sb("h_sb%d" % t, [P, S], F32) for t in range(PACK)])
         roots_in_place(last, most)
         roots_in_place(last, rest)
         scale_tiles(last, every)
-        for c in range(last):
+        for c in range(LATE):
             copy_h(c)
         make_z(last)
-        copy_h(last)
+        copy_h(LATE)
 
         out_rows = out_0.rearrange("(p t) j -> p t j", t=PACK)
         out_words = words_of(out_1)

@@ -3,7 +3,7 @@ from contextlib import ExitStack
 import concourse.mybir as mybir
 from concourse.masks import make_identity
 
-K, T, S, H, N = 512, 2048, 512, 512, 512
+T, S, H, N = 2048, 512, 512, 512
 FLOPS = 3 * 2 * 512 * 512 * 512
 
 F32 = mybir.dt.float32
@@ -20,31 +20,44 @@ P = 128
 PACK = 4
 MEMBERS = 4
 PER_COL = 16
-SPARE = 193
+HALF = S // 2
 CHUNK = 128
 CHUNKS = S // CHUNK
-VECTOR_SHARE = (2, 3, 2, 1)
-RING = 9
-FIRST_SQUARED = 2
-HALF = S // 2
-OUT_CHUNKS = (256, 128, 128)
+LAST = CHUNKS - 1
+ENTRIES = MEMBERS * CHUNK
+SPARE = 33
+VECTOR_SHARE = (2, 2, 3, 1)
 LATE = 2
+LATE_COLS = slice(LATE * CHUNK, S)
+LATE_WIDTH = S - LATE * CHUNK
+OUT_CHUNKS = (256, 128, 128)
 RUN = 4
-SCALAR_WEAVES = (0,)
 
 
 def words_of(dram_words):
     return dram_words[0].rearrange("p c r -> p (c r)").bitcast(I32)
 
 
-def load_scale_rows(queues, plane, first, dram_scales):
+def load_scale_rows(nc, plane, first, dram_scales):
     rows = dram_scales[0].bitcast(I32)
     for q in range(4):
-        queues[q].dma_start(out=plane[32 * q + first : 32 * q + first + 4, :].bitcast(I32), in_=rows[4 * q : 4 * q + 4, :])
+        nc.sync.dma_start(out=plane[32 * q + first : 32 * q + first + 4, :].bitcast(I32), in_=rows[4 * q : 4 * q + 4, :])
 
 
 def deal_columns(engine, dealt, raw):
     engine.tensor_copy(out=dealt.rearrange("p (t m) -> p t m", t=PACK), in_=raw.rearrange("p (m t) -> p t m", t=PACK))
+
+
+def by_tile(ap):
+    return ap.rearrange("p t (g i) -> p g t i", i=RUN)
+
+
+def woven(ap):
+    return ap.rearrange("p (g i) t -> p g t i", i=RUN)
+
+
+def chunk_cols(c):
+    return slice(c * CHUNK, (c + 1) * CHUNK)
 
 
 def tile_picked_mixhgsharegap_none_po_kernel(
@@ -91,13 +104,13 @@ def tile_picked_mixhgsharegap_none_po_kernel(
         for e in range(2):
             nc.sync.dma_start(out=xs[2 + e : P : 32, :].bitcast(I32), in_=x_rows[2 + e : 16 : 4, :])
         nc.sync.dma_start(out=xw[:].bitcast(I32), in_=words_of(x_words))
-        load_scale_rows((nc.sync,) * 4, w1s_raw, 0, w1_scales)
+        load_scale_rows(nc, w1s_raw, 0, w1_scales)
         nc.sync.dma_start(hz_sb[:], hz)
         nc.sync.dma_start(n1_sb[:], n1)
         nc.sync.dma_start(out=w3_raw[:].bitcast(I32), in_=words_of(w3_words))
         nc.sync.dma_start(out=w2_raw[:].bitcast(I32), in_=words_of(w2_words))
-        load_scale_rows((nc.sync,) * 4, w23s_raw, 0, w3_scales)
-        load_scale_rows((nc.sync,) * 4, w23s_raw, 4, w2_scales)
+        load_scale_rows(nc, w23s_raw, 0, w3_scales)
+        load_scale_rows(nc, w23s_raw, 4, w2_scales)
         nc.sync.dma_start(out=gn_sb[:], in_=gn.rearrange("(p t) o -> p (t o)", t=PACK))
         nc.sync.dma_start(n3_sb[:], n3)
         nc.sync.dma_start(n2_sb[:], n2)
@@ -106,7 +119,6 @@ def tile_picked_mixhgsharegap_none_po_kernel(
         for t in range(PACK):
             nc.scalar.activation(out=ex[t][:, S:], in_=zeros[:], func=ACT.Copy)
 
-        y_half = {}
         xq_s = sb("xq_s", [P, S], U8)
         first_w = sb("first_w", [P, HALF], U32)
         later_w = sb("later_w", [P, HALF + S], U32, tag="w1s_raw")
@@ -119,26 +131,27 @@ def tile_picked_mixhgsharegap_none_po_kernel(
 
         nc.vector.tensor_copy(out=xq_s[:], in_=xs[:].indirect(offs_sb[:]))
         deal_columns(nc.vector, w1[:].bitcast(I32), w1_raw[:].bitcast(I32))
+        y = {}
         for u in range(2):
-            cols = slice(u * HALF, (u + 1) * HALF)
             nc.vector.tensor_copy(out=xq_w[u], in_=xw[:].indirect(offs_sb[:, u * HALF // PER_COL : (u + 1) * HALF // PER_COL]))
             if u == 0:
                 deal_columns(nc.vector, w1s[:], w1s_raw[:])
             for pair in range(2):
-                y = psum.tile([P, 2, HALF], F32, name="y%d_%d" % (u, pair), tag="bank%d" % (2 * u + pair))
+                bank = psum.tile([P, 2, HALF], F32, name="y%d_%d" % (u, pair), tag="bank%d" % (2 * u + pair))
                 for e in range(2):
                     rows = slice((2 * pair + e) * P, (2 * pair + e + 1) * P)
                     nc.tensor.matmul_mx(
-                        out=y[:, e, :], lhsT=w1[:, rows].bitcast(FP8X4), lhsT_scale=w1s[:, rows],
-                        rhs=xq_w[u].bitcast(FP8X4), rhs_scale=xq_s[:, cols], start=True, stop=True,
+                        out=bank[:, e, :], lhsT=w1[:, rows].bitcast(FP8X4), lhsT_scale=w1s[:, rows],
+                        rhs=xq_w[u].bitcast(FP8X4), rhs_scale=xq_s[:, u * HALF : (u + 1) * HALF], start=True, stop=True,
                     )
-                y_half.setdefault((u, pair), y)
+                y.setdefault((u, pair), bank)
         for pair in range(2):
             for u in range(2):
                 for e in range(2):
                     nc.scalar.activation(
-                        out=ex[2 * pair + e][:, u * HALF : (u + 1) * HALF], in_=y_half[u, pair][:, e, :], func=ACT.Exp, scale=0.5
+                        out=ex[2 * pair + e][:, u * HALF : (u + 1) * HALF], in_=y[u, pair][:, e, :], func=ACT.Exp, scale=0.5
                     )
+
         nc.vector.tensor_copy(out=xh_w, in_=xw[:].indirect(hz_sb[:]))
         nc.vector.tensor_copy(out=xh_runs[:], in_=xs[:].indirect(hz_sb[:]))
         for e in range(2):
@@ -147,150 +160,135 @@ def tile_picked_mixhgsharegap_none_po_kernel(
 
         w23 = sb("w23", [P, 2 * N], U32, tag="xq_s")
         w3, w2 = w23[:, :N], w23[:, N:]
-        h = []
-        entries = MEMBERS * CHUNK
-        last = CHUNKS - 1
-        members = {}
+
+        terms = {}
+        root_turned = [sb("root_turned%d" % c, [P, PACK, P], F32) for c in range(LAST)]
+        share_turned = {c: sb("share_turned%d" % c, [P, PACK, P], F32) for c in range(LATE, LAST)}
         pair_sums = sb("pair_sums", [P, PACK, CHUNK, 2], F32)
-        pairs = pair_sums[:].rearrange("p t j m -> p t m j")
-        ring = []
-        root_t = [sb("root_t%d" % c, [P, PACK, P], F32) for c in range(last)]
-        den = sb("den", [P, PACK, CHUNK], F32)
-        root = {last: sb("root_last", [P, PACK, CHUNK], F32)}
-        half = [sb("half%d" % c, [P, PACK, CHUNK], F32) for c in range(CHUNKS)]
-        zi = [sb("zi%d" % c, [P, CHUNK, PACK], BF16) for c in range(CHUNKS)]
+        ms_last = sb("ms_last", [P, PACK, CHUNK], F32)
+        root_last = sb("root_last", [P, PACK, CHUNK], F32)
+        factor = {LAST: sb("share_last", [P, PACK, CHUNK], F32)}
+        scaled_early = [sb("scaled%d" % c, [P, PACK, CHUNK], F32) for c in range(LATE)]
+        scaled_late = sb("scaled_late", [P, PACK, LATE_WIDTH], F32)
+        z = [sb("z%d" % c, [P, CHUNK, PACK], BF16) for c in range(CHUNKS)]
         z_w = [sb("z_w%d" % c, [P, CHUNK], U32) for c in range(CHUNKS)]
         z_s = [sb("z_s%d" % c, [P, CHUNK], U8) for c in range(CHUNKS)]
+        h = [sb("h%d" % t, [P, S], F32) for t in range(PACK)]
         h_bank = {}
-        gained = sb("gained", [P, PACK, S - FIRST_SQUARED * CHUNK], F32)
-        share_t = {c: sb("share%d" % c, [P, PACK, CHUNK], F32) for c in range(FIRST_SQUARED, CHUNKS)}
 
         def gather_members(c):
-            window_offsets = n1_sb[:, c * entries // PER_COL : (c + 1) * entries // PER_COL]
+            offsets = n1_sb[:, c * ENTRIES // PER_COL : (c + 1) * ENTRIES // PER_COL]
             for t in range(PACK):
+                members = sb("members%d_%d" % (c, t), [P, ENTRIES], F32)
                 if t < VECTOR_SHARE[c]:
-                    unit = sb("members%d_%d" % (c, t), [P, MEMBERS, CHUNK], F32)
-                    nc.vector.tensor_copy(
-                        out=unit[:].bitcast(U32).rearrange("p m j -> p j m"), in_=ex[t][:].bitcast(U32).indirect(window_offsets)
-                    )
-                    members.setdefault((c, t), unit[:])
+                    nc.vector.tensor_copy(out=members[:], in_=ex[t][:].indirect(offsets))
                 else:
-                    unit = sb("members%d_%d" % (c, t), [P, entries], F32, tag="ring%d" % (len(ring) % RING))
-                    ring.append(unit)
-                    nc.scalar.activation(out=unit[:], in_=ex[t][:].indirect(window_offsets), func=ACT.Copy)
-                    members.setdefault((c, t), unit[:].rearrange("p (j m) -> p m j", m=MEMBERS))
+                    nc.scalar.activation(out=members[:], in_=ex[t][:].indirect(offsets), func=ACT.Copy)
+                if c < LAST and t < VECTOR_SHARE[c]:
+                    halved = sb("halved%d_%d" % (c, t), [P, ENTRIES // 2], F32)
+                    nc.gpsimd.tensor_tensor(out=halved[:], in0=members[:, 0::2], in1=members[:, 1::2], op=ALU.add)
+                    terms.setdefault((c, t), halved[:].rearrange("p (j m) -> p m j", m=2))
+                else:
+                    terms.setdefault((c, t), members[:].rearrange("p (j m) -> p m j", m=MEMBERS))
 
-        def roots_by_transposes(c):
-            total = psum.tile([P, PACK, P], F32, name="total%d" % c, tag="bank%d" % (c % 2))
+        def factor_by_transposes(c):
+            ms_turned = psum.tile([P, PACK, P], F32, name="ms_turned%d" % c, tag="bank%d" % (c % 2))
             for t in range(PACK):
-                for m in range(MEMBERS):
+                count = terms[c, t].shape[1]
+                for m in range(count):
                     nc.tensor.matmul(
-                        total[:, t, :], lhsT=members[c, t][:, m, :], rhs=ident[:],
-                        start=m == 0, stop=m == MEMBERS - 1, is_transpose=True,
+                        ms_turned[:, t, :], lhsT=terms[c, t][:, m, :], rhs=ident[:],
+                        start=m == 0, stop=m == count - 1, is_transpose=True,
                     )
-            nc.scalar.activation(out=root_t[c][:], in_=total[:], func=ACT.Abs_reciprocal_sqrt, scale=0.25, bias=0.125)
-            turned = root_t[c]
-            if c >= FIRST_SQUARED:
-                turned = share_t[c]
-                nc.scalar.activation(out=turned[:], in_=root_t[c][:], func=ACT.Square)
-            root.setdefault(c, psum.tile([P, PACK, CHUNK], F32, name="root%d" % c, tag="bank%d" % (2 + c % 2)))
+            nc.scalar.activation(out=root_turned[c][:], in_=ms_turned[:], func=ACT.Abs_reciprocal_sqrt, scale=0.25, bias=0.125)
+            turned = root_turned[c]
+            if c >= LATE:
+                turned = share_turned[c]
+                nc.scalar.activation(out=turned[:], in_=root_turned[c][:], func=ACT.Square)
+            factor.setdefault(c, psum.tile([P, PACK, CHUNK], F32, name="factor%d" % c, tag="bank%d" % (2 + c % 2)))
             for t in range(PACK):
-                nc.tensor.transpose(root[c][:, t, :], turned[:, t, :], ident[:])
+                nc.tensor.transpose(factor[c][:, t, :], turned[:, t, :], ident[:])
 
-        def roots_in_place(c, tiles):
+        def last_factor(tiles):
             for t in range(tiles.start, tiles.stop):
-                nc.vector.tensor_tensor(
-                    out=pairs[:, t, :, :].rearrange("p m j -> p j m"),
-                    in0=members[c, t][:, 0:2, :].rearrange("p m j -> p j m"),
-                    in1=members[c, t][:, 2:4, :].rearrange("p m j -> p j m"), op=ALU.add,
-                )
-            nc.vector.tensor_tensor(out=den[:, tiles, :], in0=pairs[:, tiles, 0, :], in1=pairs[:, tiles, 1, :], op=ALU.add)
-            nc.scalar.activation(out=root[c][:, tiles, :], in_=den[:, tiles, :], func=ACT.Abs_reciprocal_sqrt, scale=0.25, bias=0.125)
-            if c >= FIRST_SQUARED:
-                nc.scalar.activation(out=share_t[c][:, tiles, :], in_=root[c][:, tiles, :], func=ACT.Square)
+                quads = terms[LAST, t].rearrange("p m j -> p j m")
+                nc.vector.tensor_tensor(out=pair_sums[:, t, :, :], in0=quads[:, :, 0:2], in1=quads[:, :, 2:4], op=ALU.add)
+            nc.vector.tensor_tensor(out=ms_last[:, tiles, :], in0=pair_sums[:, tiles, :, 0], in1=pair_sums[:, tiles, :, 1], op=ALU.add)
+            nc.scalar.activation(
+                out=root_last[:, tiles, :], in_=ms_last[:, tiles, :], func=ACT.Abs_reciprocal_sqrt, scale=0.25, bias=0.125
+            )
+            nc.scalar.activation(out=factor[LAST][:, tiles, :], in_=root_last[:, tiles, :], func=ACT.Square)
 
         def h_columns(t, cols):
-            if cols.start >= LATE * CHUNK:
-                return h_bank[LATE, min(t, 2)][:, t // 3, cols.start - LATE * CHUNK : cols.stop - LATE * CHUNK]
+            if cols.start >= LATE_COLS.start:
+                return h_bank[LATE, min(t, 2)][:, t // 3, cols.start - LATE_COLS.start : cols.stop - LATE_COLS.start]
             return h_bank[cols.start // CHUNK, 0][:, t, :]
 
         def open_h(c):
             if c < LATE:
-                cols = slice(c * CHUNK, (c + 1) * CHUNK)
-                h_bank.setdefault((c, 0), psum.tile([P, PACK, CHUNK], F32, name="h%d" % c))
+                cols, openers = chunk_cols(c), (0,)
+                h_bank.setdefault((c, 0), psum.tile([P, PACK, CHUNK], F32, name="h_early%d" % c))
             else:
-                cols = slice(LATE * CHUNK, S)
+                cols, openers = LATE_COLS, (0, 1, 2)
                 for b, tag in enumerate(("h_late0", "h_late1", "bank1")):
-                    h_bank.setdefault((c, b), psum.tile([P, 2, S - LATE * CHUNK], F32, name="h_late%d" % b, tag=tag))
+                    h_bank.setdefault((c, b), psum.tile([P, 2, LATE_WIDTH], F32, name="h_late%d" % b, tag=tag))
             for t in range(PACK):
                 rows = slice(t * P, (t + 1) * P)
                 nc.tensor.matmul_mx(
                     out=h_columns(t, cols), lhsT=w3[:, rows].bitcast(FP8X4), lhsT_scale=w23s[:, rows],
-                    rhs=xh_w[:, cols].bitcast(FP8X4), rhs_scale=xh_s[:, cols], start=t == 0 or (c == LATE and t < 3), stop=False,
+                    rhs=xh_w[:, cols].bitcast(FP8X4), rhs_scale=xh_s[:, cols], start=t in openers, stop=False,
                 )
 
-        def scale_tiles(c, tiles):
-            cols = slice(c * CHUNK, (c + 1) * CHUNK)
-            for t in range(tiles.start, tiles.stop):
-                if c >= FIRST_SQUARED:
-                    continue
+        def scale_early(c):
+            for t in range(PACK):
                 nc.vector.scalar_tensor_tensor(
-                    out=half[c][:, t, :], in0=ex[t][:, cols], scalar=gn_sb[:, t : t + 1], in1=root[c][:, t, :],
-                    op0=ALU.mult, op1=ALU.mult,
+                    out=scaled_early[c][:, t, :], in0=ex[t][:, chunk_cols(c)], scalar=gn_sb[:, t : t + 1],
+                    in1=factor[c][:, t, :], op0=ALU.mult, op1=ALU.mult,
                 )
 
-        def apply_gain():
+        def scale_late():
             for t in range(PACK):
                 nc.gpsimd.tensor_scalar(
-                    out=gained[:, t, :], in0=ex[t][:, FIRST_SQUARED * CHUNK : S], scalar1=gn_sb[:, t : t + 1], scalar2=0.0, op0=ALU.mult, op1=ALU.add
+                    out=scaled_late[:, t, :], in0=ex[t][:, LATE_COLS], scalar1=gn_sb[:, t : t + 1], scalar2=0.0,
+                    op0=ALU.mult, op1=ALU.add,
                 )
 
         def make_z(c):
-            nc.vector.tensor_tensor(
-                out=zi[c][:].rearrange("p (g i) t -> p g t i", i=RUN),
-                in0=(half[c][:] if c < FIRST_SQUARED else gained[:, :, (c - FIRST_SQUARED) * CHUNK : (c - FIRST_SQUARED + 1) * CHUNK]).rearrange("p t (g i) -> p g t i", i=RUN),
-                in1=(share_t[c] if c == last and c >= FIRST_SQUARED else root[c])[:].rearrange("p t (g i) -> p g t i", i=RUN),
-                op=ALU.mult,
-            )
-            nc.vector.quantize_mx(out=z_w[c][:].bitcast(FP8X4), scales=z_s[c][:], in_=zi[c][:].rearrange("p j t -> p (j t)"))
+            scaled = scaled_early[c][:] if c < LATE else scaled_late[:, :, chunk_cols(c - LATE)]
+            nc.vector.tensor_tensor(out=woven(z[c][:]), in0=by_tile(scaled), in1=by_tile(factor[c][:]), op=ALU.mult)
+            nc.vector.quantize_mx(out=z_w[c][:].bitcast(FP8X4), scales=z_s[c][:], in_=z[c][:].rearrange("p j t -> p (j t)"))
+            closers = (PACK - 1,) if c < LATE else (0, 1, 3) if c == LAST else ()
             for t in range(PACK):
                 rows = slice(t * P, (t + 1) * P)
                 nc.tensor.matmul_mx(
-                    out=h_columns(t, slice(c * CHUNK, (c + 1) * CHUNK)), lhsT=w2[:, rows].bitcast(FP8X4), lhsT_scale=w23s[4:P, rows],
-                    rhs=z_w[c][:].bitcast(FP8X4), rhs_scale=z_s[c][:], start=False, stop=(t != 2 if c == last else c < LATE and t == PACK - 1),
+                    out=h_columns(t, chunk_cols(c)), lhsT=w2[:, rows].bitcast(FP8X4), lhsT_scale=w23s[4:P, rows],
+                    rhs=z_w[c][:].bitcast(FP8X4), rhs_scale=z_s[c][:], start=False, stop=t in closers,
                 )
 
-        def copy_h(c):
-            cols = slice(c * CHUNK, (c + 1) * CHUNK if c < LATE else S)
-            for t in range(PACK):
-                if c == LATE and t >= 1:
-                    nc.vector.tensor_copy(out=h[t][:, cols], in_=h_columns(t, cols))
-                else:
-                    nc.scalar.copy(out=h[t][:, cols], in_=h_columns(t, cols))
-
-        every, most, rest = slice(0, PACK), slice(0, PACK - 1), slice(PACK - 1, PACK)
         gather_members(0)
         gather_members(1)
         deal_columns(nc.gpsimd, w3.bitcast(I32), w3_raw[:].bitcast(I32))
         deal_columns(nc.gpsimd, w23s[:], w23s_raw[:])
         deal_columns(nc.gpsimd, w2.bitcast(I32), w2_raw[:].bitcast(I32))
-        for c in range(last):
-            roots_by_transposes(c)
+        for c in range(LAST):
+            factor_by_transposes(c)
             open_h(c)
             if c + 2 < CHUNKS:
                 gather_members(c + 2)
-            scale_tiles(c, every)
+            if c < LATE:
+                scale_early(c)
             if c == 0:
-                apply_gain()
+                scale_late()
             make_z(c)
-        h.extend([sb("h_sb%d" % t, [P, S], F32) for t in range(PACK)])
-        roots_in_place(last, most)
-        roots_in_place(last, rest)
-        scale_tiles(last, every)
+        last_factor(slice(0, PACK - 1))
+        last_factor(slice(PACK - 1, PACK))
         for c in range(LATE):
-            copy_h(c)
-        make_z(last)
-        copy_h(LATE)
+            for t in range(PACK):
+                nc.scalar.copy(out=h[t][:, chunk_cols(c)], in_=h_columns(t, chunk_cols(c)))
+        make_z(LAST)
+        nc.scalar.copy(out=h[0][:, LATE_COLS], in_=h_columns(0, LATE_COLS))
+        for t in range(1, PACK):
+            nc.vector.tensor_copy(out=h[t][:, LATE_COLS], in_=h_columns(t, LATE_COLS))
 
         out_rows = out_0.rearrange("(p t) j -> p t j", t=PACK)
         out_words = words_of(out_1)
@@ -299,24 +297,22 @@ def tile_picked_mixhgsharegap_none_po_kernel(
         for c, width in enumerate(OUT_CHUNKS):
             first = sum(OUT_CHUNKS[:c])
             cols = slice(first, first + width)
-            lists = slice(first // PER_COL, (first + width) // PER_COL)
+            entries = slice(first // PER_COL, (first + width) // PER_COL)
             less = sb("less%d" % c, [P, PACK, width], F32)
             gap = sb("gap%d" % c, [P, PACK, width], F32)
             for t in range(PACK):
-                nc.scalar.activation(out=less[:, t, :], in_=h[t][:].indirect(n3_sb[:, lists]), func=ACT.Copy)
-                nc.vector.tensor_tensor(out=gap[:, t, :], in0=h[t][:].indirect(n2_sb[:, lists]), in1=less[:, t, :], op=ALU.subtract)
+                nc.scalar.activation(out=less[:, t, :], in_=h[t][:].indirect(n3_sb[:, entries]), func=ACT.Copy)
+                nc.vector.tensor_tensor(out=gap[:, t, :], in0=h[t][:].indirect(n2_sb[:, entries]), in1=less[:, t, :], op=ALU.subtract)
             nc.sync.dma_start(out=out_rows[:, :, cols], in_=gap[:])
             gaps.append((cols, width, gap))
         for c, (cols, width, gap) in enumerate(gaps):
-            gap_i = sb("gap_i%d" % c, [P, width, PACK], BF16)
+            rounded = sb("rounded%d" % c, [P, width, PACK], BF16)
             o_w = sb("o_w%d" % c, [P, width], U32)
-            woven = gap_i[:].rearrange("p (g i) t -> p g t i", i=RUN)
-            source = gap[:].rearrange("p t (g i) -> p g t i", i=RUN)
-            if c in SCALAR_WEAVES:
-                nc.scalar.copy(out=woven, in_=source)
+            if c == 0:
+                nc.scalar.copy(out=woven(rounded[:]), in_=by_tile(gap[:]))
             else:
-                nc.vector.tensor_copy(out=woven, in_=source)
-            nc.vector.quantize_mx(out=o_w[:].bitcast(FP8X4), scales=o_s[:, cols], in_=gap_i[:].rearrange("p j t -> p (j t)"))
+                nc.vector.tensor_copy(out=woven(rounded[:]), in_=by_tile(gap[:]))
+            nc.vector.quantize_mx(out=o_w[:].bitcast(FP8X4), scales=o_s[:, cols], in_=rounded[:].rearrange("p j t -> p (j t)"))
             nc.sync.dma_start(out=out_words[:, cols], in_=o_w[:].bitcast(I32))
         scale_rows = out_2[0].bitcast(I32)
         for q in range(4):

from contextlib import ExitStack

import concourse.mybir as mybir
from concourse.masks import make_identity

T, S, H, N = 2048, 512, 512, 512
FLOPS = 3 * 2 * 512 * 512 * 512

F32 = mybir.dt.float32
BF16 = mybir.dt.bfloat16
I32 = mybir.dt.int32
U32 = mybir.dt.uint32
U16 = mybir.dt.uint16
U8 = mybir.dt.uint8
FP8X4 = mybir.dt.float8_e4m3fn_x4
ACT = mybir.ActivationFunctionType
ALU = mybir.AluOpType

P = 128
PACK = 4
MEMBERS = 4
PER_COL = 16
HALF = S // 2
CHUNK = 128
CHUNKS = S // CHUNK
LAST = CHUNKS - 1
ENTRIES = MEMBERS * CHUNK
SPARE = 33
VECTOR_SHARE = (2, 2, 3, 1)
LATE = 2
LATE_COLS = slice(LATE * CHUNK, S)
LATE_WIDTH = S - LATE * CHUNK
OUT_CHUNKS = (256, 128, 128)
RUN = 4


def words_of(dram_words):
    return dram_words[0].rearrange("p c r -> p (c r)").bitcast(I32)


def load_scale_rows(nc, plane, first, dram_scales):
    rows = dram_scales[0].bitcast(I32)
    for q in range(4):
        nc.sync.dma_start(out=plane[32 * q + first : 32 * q + first + 4, :].bitcast(I32), in_=rows[4 * q : 4 * q + 4, :])


def deal_columns(engine, dealt, raw):
    engine.tensor_copy(out=dealt.rearrange("p (t m) -> p t m", t=PACK), in_=raw.rearrange("p (m t) -> p t m", t=PACK))


def by_tile(ap):
    return ap.rearrange("p t (g i) -> p g t i", i=RUN)


def woven(ap):
    return ap.rearrange("p (g i) t -> p g t i", i=RUN)


def chunk_cols(c):
    return slice(c * CHUNK, (c + 1) * CHUNK)


def tile_picked_mixhgsharegap_none_po_kernel(
    tc, x_words, x_scales, w1_words, w1_scales, gn, w2_words, w2_scales, w3_words, w3_scales,
    offs, n1, hz, n2, n3, out_0, out_1, out_2,
):
    nc = tc.nc
    with ExitStack() as ctx:
        keep = ctx.enter_context(tc.tile_pool(name="keep", bufs=1))
        psum = ctx.enter_context(tc.psum_pool(name="psum", bufs=1))

        def sb(name, shape, dtype, tag=None):
            return keep.tile(shape, dtype, name=name, tag=tag or name, align_bytes=64)

        offs_sb = sb("offs_sb", [P, S // PER_COL], U16)
        hz_sb = sb("hz_sb", [P, S // PER_COL], U16)
        n1_sb = sb("n1_sb", [P, MEMBERS * S // PER_COL], U16)
        n2_sb = sb("n2_sb", [P, S // PER_COL], U16)
        n3_sb = sb("n3_sb", [P, S // PER_COL], U16)
        xw = sb("xw", [P, T], U32)
        xs = sb("xs", [P, T], U8)
        w1_raw = sb("w1_raw", [P, H], U32)
        w2_raw = sb("w2_raw", [P, N], U32)
        w3_raw = sb("w3_raw", [P, N], U32)
        w1s_raw = sb("w1s_raw", [P, H], U8)
        w23s_raw = sb("w23s_raw", [P, N], U8)
        xh_s = sb("xh_s", [P, S], U8)
        gn_sb = sb("gn_sb", [P, PACK], F32)
        zeros = sb("zeros", [P, SPARE], F32)
        ident = sb("ident", [P, P], F32)

        nc.vector.memset(xs[:].bitcast(I32), 0)
        nc.vector.memset(zeros[:], 0.0)
        nc.gpsimd.memset(w1s_raw[:].bitcast(I32), 0)
        nc.gpsimd.memset(w23s_raw[:].bitcast(I32), 0)
        nc.gpsimd.memset(xh_s[:].bitcast(I32), 0)
        make_identity(nc, ident[:])

        x_rows = x_scales[0].bitcast(I32)
        nc.sync.dma_start(offs_sb[:], offs)
        nc.sync.dma_start(out=w1_raw[:].bitcast(I32), in_=words_of(w1_words))
        for e in range(2):
            nc.scalar.dma_start(out=xs[e:P:16, :].bitcast(I32), in_=x_rows[e:16:2, :])
        for e in range(2):
            nc.sync.dma_start(out=xs[2 + e : P : 32, :].bitcast(I32), in_=x_rows[2 + e : 16 : 4, :])
        nc.sync.dma_start(out=xw[:].bitcast(I32), in_=words_of(x_words))
        load_scale_rows(nc, w1s_raw, 0, w1_scales)
        nc.sync.dma_start(hz_sb[:], hz)
        nc.sync.dma_start(n1_sb[:], n1)
        nc.sync.dma_start(out=w3_raw[:].bitcast(I32), in_=words_of(w3_words))
        nc.sync.dma_start(out=w2_raw[:].bitcast(I32), in_=words_of(w2_words))
        load_scale_rows(nc, w23s_raw, 0, w3_scales)
        load_scale_rows(nc, w23s_raw, 4, w2_scales)
        nc.sync.dma_start(out=gn_sb[:], in_=gn.rearrange("(p t) o -> p (t o)", t=PACK))
        nc.sync.dma_start(n3_sb[:], n3)
        nc.sync.dma_start(n2_sb[:], n2)

        ex = [sb("ex%d" % t, [P, S + SPARE], F32) for t in range(PACK)]
        for t in range(PACK):
            nc.scalar.activation(out=ex[t][:, S:], in_=zeros[:], func=ACT.Copy)

        xq_s = sb("xq_s", [P, S], U8)
        first_w = sb("first_w", [P, HALF], U32)
        later_w = sb("later_w", [P, HALF + S], U32, tag="w1s_raw")
        xq_w = (first_w[:], later_w[:, :HALF])
        xh_w = later_w[:, HALF:]
        xh_runs = sb("xh_runs", [P, S], U8, tag="first_w")
        w1 = sb("w1", [P, H], U32)
        w1s = sb("w1s", [P, H], U8)
        w23s = sb("w23s", [P, N], U8)

        nc.vector.tensor_copy(out=xq_s[:], in_=xs[:].indirect(offs_sb[:]))
        deal_columns(nc.vector, w1[:].bitcast(I32), w1_raw[:].bitcast(I32))
        y = {}
        for u in range(2):
            nc.vector.tensor_copy(out=xq_w[u], in_=xw[:].indirect(offs_sb[:, u * HALF // PER_COL : (u + 1) * HALF // PER_COL]))
            if u == 0:
                deal_columns(nc.vector, w1s[:], w1s_raw[:])
            for pair in range(2):
                bank = psum.tile([P, 2, HALF], F32, name="y%d_%d" % (u, pair), tag="bank%d" % (2 * u + pair))
                for e in range(2):
                    rows = slice((2 * pair + e) * P, (2 * pair + e + 1) * P)
                    nc.tensor.matmul_mx(
                        out=bank[:, e, :], lhsT=w1[:, rows].bitcast(FP8X4), lhsT_scale=w1s[:, rows],
                        rhs=xq_w[u].bitcast(FP8X4), rhs_scale=xq_s[:, u * HALF : (u + 1) * HALF], start=True, stop=True,
                    )
                y.setdefault((u, pair), bank)
        for pair in range(2):
            for u in range(2):
                for e in range(2):
                    nc.scalar.activation(
                        out=ex[2 * pair + e][:, u * HALF : (u + 1) * HALF], in_=y[u, pair][:, e, :], func=ACT.Exp, scale=0.5
                    )

        nc.vector.tensor_copy(out=xh_w, in_=xw[:].indirect(hz_sb[:]))
        nc.vector.tensor_copy(out=xh_runs[:], in_=xs[:].indirect(hz_sb[:]))
        for e in range(2):
            nc.sync.dma_start(out=xh_s[e:P:32, :].bitcast(I32), in_=xh_runs[e:P:32, :].bitcast(I32))
            nc.sync.dma_start(out=xh_s[2 + e : P : 32, :].bitcast(I32), in_=xh_runs[16 + e : P : 32, :].bitcast(I32))

        w23 = sb("w23", [P, 2 * N], U32, tag="xq_s")
        w3, w2 = w23[:, :N], w23[:, N:]

        terms = {}
        root_turned = [sb("root_turned%d" % c, [P, PACK, P], F32) for c in range(LAST)]
        share_turned = {c: sb("share_turned%d" % c, [P, PACK, P], F32) for c in range(LATE, LAST)}
        pair_sums = sb("pair_sums", [P, PACK, CHUNK, 2], F32)
        ms_last = sb("ms_last", [P, PACK, CHUNK], F32)
        root_last = sb("root_last", [P, PACK, CHUNK], F32)
        factor = {LAST: sb("share_last", [P, PACK, CHUNK], F32)}
        scaled_early = [sb("scaled%d" % c, [P, PACK, CHUNK], F32) for c in range(LATE)]
        scaled_late = sb("scaled_late", [P, PACK, LATE_WIDTH], F32)
        z = [sb("z%d" % c, [P, CHUNK, PACK], BF16) for c in range(CHUNKS)]
        z_w = [sb("z_w%d" % c, [P, CHUNK], U32) for c in range(CHUNKS)]
        z_s = [sb("z_s%d" % c, [P, CHUNK], U8) for c in range(CHUNKS)]
        h = [sb("h%d" % t, [P, S], F32) for t in range(PACK)]
        h_bank = {}

        def gather_members(c):
            offsets = n1_sb[:, c * ENTRIES // PER_COL : (c + 1) * ENTRIES // PER_COL]
            for t in range(PACK):
                members = sb("members%d_%d" % (c, t), [P, ENTRIES], F32)
                if t < VECTOR_SHARE[c]:
                    nc.vector.tensor_copy(out=members[:], in_=ex[t][:].indirect(offsets))
                else:
                    nc.scalar.activation(out=members[:], in_=ex[t][:].indirect(offsets), func=ACT.Copy)
                if c < LAST and t < VECTOR_SHARE[c]:
                    halved = sb("halved%d_%d" % (c, t), [P, ENTRIES // 2], F32)
                    nc.gpsimd.tensor_tensor(out=halved[:], in0=members[:, 0::2], in1=members[:, 1::2], op=ALU.add)
                    terms.setdefault((c, t), halved[:].rearrange("p (j m) -> p m j", m=2))
                else:
                    terms.setdefault((c, t), members[:].rearrange("p (j m) -> p m j", m=MEMBERS))

        def factor_by_transposes(c):
            ms_turned = psum.tile([P, PACK, P], F32, name="ms_turned%d" % c, tag="bank%d" % (c % 2))
            for t in range(PACK):
                count = terms[c, t].shape[1]
                for m in range(count):
                    nc.tensor.matmul(
                        ms_turned[:, t, :], lhsT=terms[c, t][:, m, :], rhs=ident[:],
                        start=m == 0, stop=m == count - 1, is_transpose=True,
                    )
            nc.scalar.activation(out=root_turned[c][:], in_=ms_turned[:], func=ACT.Abs_reciprocal_sqrt, scale=0.25, bias=0.125)
            turned = root_turned[c]
            if c >= LATE:
                turned = share_turned[c]
                nc.scalar.activation(out=turned[:], in_=root_turned[c][:], func=ACT.Square)
            factor.setdefault(c, psum.tile([P, PACK, CHUNK], F32, name="factor%d" % c, tag="bank%d" % (2 + c % 2)))
            for t in range(PACK):
                nc.tensor.transpose(factor[c][:, t, :], turned[:, t, :], ident[:])

        def last_factor(tiles):
            for t in range(tiles.start, tiles.stop):
                quads = terms[LAST, t].rearrange("p m j -> p j m")
                nc.vector.tensor_tensor(out=pair_sums[:, t, :, :], in0=quads[:, :, 0:2], in1=quads[:, :, 2:4], op=ALU.add)
            nc.vector.tensor_tensor(out=ms_last[:, tiles, :], in0=pair_sums[:, tiles, :, 0], in1=pair_sums[:, tiles, :, 1], op=ALU.add)
            nc.scalar.activation(
                out=root_last[:, tiles, :], in_=ms_last[:, tiles, :], func=ACT.Abs_reciprocal_sqrt, scale=0.25, bias=0.125
            )
            nc.scalar.activation(out=factor[LAST][:, tiles, :], in_=root_last[:, tiles, :], func=ACT.Square)

        def h_columns(t, cols):
            if cols.start >= LATE_COLS.start:
                return h_bank[LATE, min(t, 2)][:, t // 3, cols.start - LATE_COLS.start : cols.stop - LATE_COLS.start]
            return h_bank[cols.start // CHUNK, 0][:, t, :]

        def open_h(c):
            if c < LATE:
                cols, openers = chunk_cols(c), (0,)
                h_bank.setdefault((c, 0), psum.tile([P, PACK, CHUNK], F32, name="h_early%d" % c))
            else:
                cols, openers = LATE_COLS, (0, 1, 2)
                for b, tag in enumerate(("h_late0", "h_late1", "bank1")):
                    h_bank.setdefault((c, b), psum.tile([P, 2, LATE_WIDTH], F32, name="h_late%d" % b, tag=tag))
            for t in range(PACK):
                rows = slice(t * P, (t + 1) * P)
                nc.tensor.matmul_mx(
                    out=h_columns(t, cols), lhsT=w3[:, rows].bitcast(FP8X4), lhsT_scale=w23s[:, rows],
                    rhs=xh_w[:, cols].bitcast(FP8X4), rhs_scale=xh_s[:, cols], start=t in openers, stop=False,
                )

        def scale_early(c):
            for t in range(PACK):
                nc.vector.scalar_tensor_tensor(
                    out=scaled_early[c][:, t, :], in0=ex[t][:, chunk_cols(c)], scalar=gn_sb[:, t : t + 1],
                    in1=factor[c][:, t, :], op0=ALU.mult, op1=ALU.mult,
                )

        def scale_late():
            for t in range(PACK):
                nc.gpsimd.tensor_scalar(
                    out=scaled_late[:, t, :], in0=ex[t][:, LATE_COLS], scalar1=gn_sb[:, t : t + 1], scalar2=0.0,
                    op0=ALU.mult, op1=ALU.add,
                )

        def make_z(c):
            scaled = scaled_early[c][:] if c < LATE else scaled_late[:, :, chunk_cols(c - LATE)]
            nc.vector.tensor_tensor(out=woven(z[c][:]), in0=by_tile(scaled), in1=by_tile(factor[c][:]), op=ALU.mult)
            nc.vector.quantize_mx(out=z_w[c][:].bitcast(FP8X4), scales=z_s[c][:], in_=z[c][:].rearrange("p j t -> p (j t)"))
            closers = (PACK - 1,) if c < LATE else (0, 1, 3) if c == LAST else ()
            for t in range(PACK):
                rows = slice(t * P, (t + 1) * P)
                nc.tensor.matmul_mx(
                    out=h_columns(t, chunk_cols(c)), lhsT=w2[:, rows].bitcast(FP8X4), lhsT_scale=w23s[4:P, rows],
                    rhs=z_w[c][:].bitcast(FP8X4), rhs_scale=z_s[c][:], start=False, stop=t in closers,
                )

        gather_members(0)
        gather_members(1)
        deal_columns(nc.gpsimd, w3.bitcast(I32), w3_raw[:].bitcast(I32))
        deal_columns(nc.gpsimd, w23s[:], w23s_raw[:])
        deal_columns(nc.gpsimd, w2.bitcast(I32), w2_raw[:].bitcast(I32))
        for c in range(LAST):
            factor_by_transposes(c)
            open_h(c)
            if c + 2 < CHUNKS:
                gather_members(c + 2)
            if c < LATE:
                scale_early(c)
            if c == 0:
                scale_late()
            make_z(c)
        last_factor(slice(0, PACK - 1))
        last_factor(slice(PACK - 1, PACK))
        for c in range(LATE):
            for t in range(PACK):
                nc.scalar.copy(out=h[t][:, chunk_cols(c)], in_=h_columns(t, chunk_cols(c)))
        make_z(LAST)
        nc.scalar.copy(out=h[0][:, LATE_COLS], in_=h_columns(0, LATE_COLS))
        for t in range(1, PACK):
            nc.vector.tensor_copy(out=h[t][:, LATE_COLS], in_=h_columns(t, LATE_COLS))

        out_rows = out_0.rearrange("(p t) j -> p t j", t=PACK)
        out_words = words_of(out_1)
        o_s = sb("o_s", [P, S], U8)
        gaps = []
        for c, width in enumerate(OUT_CHUNKS):
            first = sum(OUT_CHUNKS[:c])
            cols = slice(first, first + width)
            entries = slice(first // PER_COL, (first + width) // PER_COL)
            less = sb("less%d" % c, [P, PACK, width], F32)
            gap = sb("gap%d" % c, [P, PACK, width], F32)
            for t in range(PACK):
                nc.scalar.activation(out=less[:, t, :], in_=h[t][:].indirect(n3_sb[:, entries]), func=ACT.Copy)
                nc.vector.tensor_tensor(out=gap[:, t, :], in0=h[t][:].indirect(n2_sb[:, entries]), in1=less[:, t, :], op=ALU.subtract)
            nc.sync.dma_start(out=out_rows[:, :, cols], in_=gap[:])
            gaps.append((cols, width, gap))
        for c, (cols, width, gap) in enumerate(gaps):
            rounded = sb("rounded%d" % c, [P, width, PACK], BF16)
            o_w = sb("o_w%d" % c, [P, width], U32)
            if c == 0:
                nc.scalar.copy(out=woven(rounded[:]), in_=by_tile(gap[:]))
            else:
                nc.vector.tensor_copy(out=woven(rounded[:]), in_=by_tile(gap[:]))
            nc.vector.quantize_mx(out=o_w[:].bitcast(FP8X4), scales=o_s[:, cols], in_=rounded[:].rearrange("p j t -> p (j t)"))
            nc.sync.dma_start(out=out_words[:, cols], in_=o_w[:].bitcast(I32))
        scale_rows = out_2[0].bitcast(I32)
        for q in range(4):
            queue = nc.sync if q % 2 == 0 else nc.scalar
            queue.dma_start(out=scale_rows[4 * q : 4 * q + 4, :], in_=o_s[32 * q : 32 * q + 4, :].bitcast(I32))
